import numpy as np, ml_dtypes
CORES = [5,21,45,77,85,101,109,125,133,141,189,213]
N = 12
import mx_ref
NC, KB = 128, 1
BF = ml_dtypes.bfloat16
def cut(t, i, w=512):
    return t[:, w * i:w * i + w]
def term(a, B):
    return np.stack([mx_ref.matmul(mx_ref.quantize(cut(a, i)), B) for i in range(4)], axis=2).reshape(128, -1)
def setup_inputs(rng):
    def f(*shape):
        return mx_ref.flush((rng.standard_normal(shape, dtype=np.float32) * np.exp2(rng.integers(-2, 3, shape[:-1] + (1,)))).astype(BF))
    return {"a": f(N, 128, 4 * 512), "b": f(N, 128, KB * 4 * NC)}
def setup_inputs_blocks(rng):
    d = setup_inputs(rng)
    for k in ("a", "b"): d[k] = mx_ref.spread(d[k], rng, 2)
    return d
def setup_inputs_wide(rng):
    d = setup_inputs(rng)
    for k in ("a", "b"): d[k] = mx_ref.flush((d[k].astype(np.float32) * np.exp2(rng.integers(-4, 5, (N, 1, 1))).astype(np.float32)).astype(BF))
    return d
def setup_inputs_lossless(rng):
    a = np.zeros((N, 128, 4 * 128, 4), np.float32)
    for r in range(N):
        k = rng.integers(0, 512, size=4 * 128)
        a[r, k // 4, np.arange(4 * 128), k % 4] = 1.0
    size = np.repeat(2.0 ** rng.integers(-4, 5, size=(1, 1, (KB * 4 * NC) // 4)), 4, axis=2)
    b = rng.integers(-1, 2, size=(N, 128, KB * 4 * NC)) * size
    return {"a": a.reshape(N, 128, 4 * 512).astype(BF), "b": b.astype(np.float32).astype(BF)}
def reference(a, b):
    y = np.zeros((N, 128, KB * 4 * NC), np.float32)
    for k in range(KB):
        y[:, :, 4 * NC * k:4 * NC * k + 4 * NC] = mx_ref.total([term(a[r], mx_ref.quantize(cut(b[r], k, 4 * NC))) for r in range(N)])
    return {"y": y}

@@ -1,0 +1,208 @@
+from concourse.bass import DstId, RemoteDMATransfer
+from concourse.mybir import dt, AluOpType, ActivationFunctionType
+
+N = 12
+SIM_CORES = 256
+W = 128
+NRELAY = 2
+
+SCRATCH = {
+    "a_sb": ("sbuf", [128, 2048], "bfloat16"),
+    "b_sb": ("sbuf", [128, 512], "bfloat16"),
+    "qa": ("sbuf", [128, 512], "float8_e4m3fn_x4"),
+    "sa": ("sbuf", [128, 512], "uint8"),
+    "qb": ("sbuf", [128, 128], "float8_e4m3fn_x4"),
+    "sb": ("sbuf", [128, 128], "uint8"),
+    "ones": ("sbuf", [128, 516], "bfloat16"),
+    "z": ("sbuf", [128, 516], "bfloat16"),
+    "qs": ("sbuf", [128, 512], "float8_e4m3fn_x4"),
+    "ss": ("sbuf", [128, 512], "uint8"),
+    "t_sb": ("sbuf", [128, 512], "bfloat16"),
+    "qt": ("sbuf", [128, 128], "float8_e4m3fn_x4"),
+    "st": ("sbuf", [128, 128], "uint8"),
+    "rq": ("sbuf", [128, 128], "float8_e4m3fn_x4"),
+    "rs": ("sbuf", [128, 128], "uint8"),
+    "land_q": ("sbuf", [128, N * 128], "float8_e4m3fn_x4"),
+    "land_s": ("sbuf", [128, N * 128], "uint8"),
+    "y_sb": ("sbuf", [128, 512], "float32"),
+    "pp": ("psum", [128, 2048], "float32"),
+    "acc": ("psum", [128, 2048], "float32"),
+}
+SEMAPHORES = (["ld_b", "q_b", "ones_ok", "z_ok", "cp", "q_t", "q_s", "rel_s", "rel_q", "sent", "yc", "stored"]
+              + ["ld_a%d" % i for i in range(4)] + ["q_a%d" % i for i in range(4)]
+              + ["pm%d" % i for i in range(4)] + ["fin%d" % i for i in range(4)]
+              + ["arr%d" % r for r in range(N)])
+
+
+def _count(mask):
+    return bin(mask).count("1")
+
+
+def _plan(T, topo, r):
+    me = T.cores[r]
+    near = [d for d in range(N) if d == r or topo.may_write(me, T.cores[d])]
+    far = [d for d in range(N) if d not in near]
+    k = near.index(r)
+    direct = [near[(k + j) % len(near)] for j in range(1, len(near))]
+    far = [far[(k + j) % len(far)] for j in range(len(far))]
+    chip = [c for c in range(SIM_CORES)
+            if c != me and topo.host(c) == topo.host(me) and topo.chip(c) == topo.chip(me)]
+    able = [c for c in chip if all(topo.may_write(c, T.cores[d]) for d in far)]
+    able.sort(key=lambda c: (topo.die(c) == topo.die(me), c))
+    relays = able[:NRELAY] if far else []
+    share = (len(far) + len(relays) - 1) // len(relays) if relays else 0
+    return direct, [(c, far[share * x:share * x + share]) for x, c in enumerate(relays)]
+
+
+def _common_mask(topo, src, dsts):
+    m = topo.mask(src, dsts[0])
+    for d in dsts[1:]:
+        m &= topo.mask(src, d)
+    return m
+
+
+def _ids(topo, src, dsts):
+    out = []
+    for d in dsts:
+        rid, pid = topo.addr(d, src)
+        out.append(DstId(rid=rid, pnc=pid))
+    return out
+
+
+def _relay_program(g, core, T, topo, r, dests, n_in):
+    cores = [T.cores[d] for d in dests]
+    m = _common_mask(topo, core, cores)
+    ids = _ids(topo, core, cores)
+    sl = slice(W * r, W * r + W)
+    g.wait_ge(T.sem.rel_s, n_in)
+    g.remote_dma_fused([RemoteDMATransfer(dst_ids=ids, dma_engine_mask=m, remote_sem=T.sem["arr%d" % r],
+                                          srcs=[T.rs[:]], dsts=[T.land_s[:, sl] for _ in dests])],
+                       local_sem=T.sem.sent)
+    g.wait_ge(T.sem.rel_q, n_in)
+    g.remote_dma_fused([RemoteDMATransfer(dst_ids=ids, dma_engine_mask=m, remote_sem=T.sem["arr%d" % r],
+                                          srcs=[T.rq[:].bitcast(dt.uint8)],
+                                          dsts=[T.land_q[:, sl].bitcast(dt.uint8) for _ in dests])],
+                       local_sem=T.sem.sent)
+    g.wait_ge(T.sem.sent, 2 * _count(m))
+
+
+def rank_program(g, core, T, topo):
+    rank = T.rank_of(core)
+    plans = [_plan(T, topo, r) for r in range(N)]
+
+    def masks(r):
+        me = T.cores[r]
+        direct, relays = plans[r]
+        lo = _common_mask(topo, me, [T.cores[d] for d in direct])
+        on = _common_mask(topo, me, [c for c, _ in relays])
+        hi = on & ~lo
+        return lo, (hi if hi else on)
+
+    if rank is None:
+        for r in range(N):
+            for c, dests in plans[r][1]:
+                if c == core:
+                    _relay_program(g, core, T, topo, r, dests, _count(masks(r)[1]))
+        return
+
+    v, te, sc, sy = g.vector, g.tensor, g.scalar, g.sync
+    S = T.sem
+
+    sy.dma_start(T.b_sb[:], T.b[:]).then_inc(S.ld_b, 16)
+    for i in range(4):
+        q = sc if i % 2 == 0 else sy
+        q.dma_start(T.a_sb[:, 512 * i:512 * i + 512], T.a[:, 512 * i:512 * i + 512]).then_inc(S["ld_a%d" % i], 16)
+
+    v.memset(T.ones[:], 1.0).then_inc(S.ones_ok, 1)
+    g.wait_ge(S.ones_ok, 1)
+    g.affine_select(T.z[:], T.ones[:], [[-1, 516]], AluOpType.is_equal, 0.0, 3, 4).then_inc(S.z_ok, 1)
+
+    def quant_a(i):
+        v.wait_ge(S["ld_a%d" % i], 16)
+        v.quantize_mx(T.qa[:, W * i:W * i + W], T.sa[:, W * i:W * i + W],
+                      T.a_sb[:, 512 * i:512 * i + 512]).then_inc(S["q_a%d" % i], 1)
+
+    def copy_p(i):
+        v.wait_ge(S["pm%d" % i], 1)
+        v.tensor_copy(T.t_sb[:, i:512:4], T.pp[:, 512 * i:512 * i + W]).then_inc(S.cp, 1)
+
+    v.wait_ge(S.ld_b, 16)
+    v.quantize_mx(T.qb[:], T.sb[:], T.b_sb[:]).then_inc(S.q_b, 1)
+    quant_a(0)
+    quant_a(1)
+    copy_p(0)
+    quant_a(2)
+    copy_p(1)
+    quant_a(3)
+    copy_p(2)
+    copy_p(3)
+    v.wait_ge(S.cp, 4)
+    v.quantize_mx(T.qt[:], T.st[:], T.t_sb[:]).then_inc(S.q_t, 1)
+    v.wait_ge(S.z_ok, 1)
+    for i in range(4):
+        v.quantize_mx(T.qs[:, W * i:W * i + W], T.ss[:, W * i:W * i + W], T.z[:, 3 - i:3 - i + 512]).then_inc(S.q_s, 1)
+
+    def product(out, i, stop):
+        return te.matmul_mx(out[:, 512 * i:512 * i + W], T.qa[:, W * i:W * i + W], T.sa[:, W * i:W * i + W],
+                            T.qb[:], T.sb[:], True, stop)
+
+    te.wait_ge(S.q_b, 1)
+    for i in range(4):
+        te.wait_ge(S["q_a%d" % i], 1)
+        product(T.pp, i, True).then_inc(S["pm%d" % i], 1)
+    for i in range(4):
+        product(T.acc, i, False)
+
+    direct, relays = plans[rank]
+    lo, hi = masks(rank)
+    sl = slice(W * rank, W * rank + W)
+    dcores = [T.cores[d] for d in direct]
+    rcores = [c for c, _ in relays]
+    g.wait_ge(S.q_t, 1)
+    g.remote_dma_fused([
+        RemoteDMATransfer(dst_ids=_ids(topo, core, rcores), dma_engine_mask=hi, remote_sem=S.rel_s,
+                          srcs=[T.st[:]], dsts=[T.rs[:] for _ in rcores]),
+        RemoteDMATransfer(dst_ids=_ids(topo, core, dcores), dma_engine_mask=lo, remote_sem=S["arr%d" % rank],
+                          srcs=[T.st[:]], dsts=[T.land_s[:, sl] for _ in dcores]),
+    ], local_sem=S.sent)
+    g.remote_dma_fused([
+        RemoteDMATransfer(dst_ids=_ids(topo, core, rcores), dma_engine_mask=hi, remote_sem=S.rel_q,
+                          srcs=[T.qt[:].bitcast(dt.uint8)], dsts=[T.rq[:].bitcast(dt.uint8) for _ in rcores]),
+        RemoteDMATransfer(dst_ids=_ids(topo, core, dcores), dma_engine_mask=lo, remote_sem=S["arr%d" % rank],
+                          srcs=[T.qt[:].bitcast(dt.uint8)], dsts=[T.land_q[:, sl].bitcast(dt.uint8) for _ in dcores]),
+    ], local_sem=S.sent)
+
+    expect = []
+    for r in range(N):
+        if r == rank:
+            continue
+        d_r, rel_r = plans[r]
+        if rank in d_r:
+            expect.append(((0, d_r.index(rank), 0), r, 2 * _count(masks(r)[0])))
+        for x, (c, dests) in enumerate(rel_r):
+            if rank in dests:
+                m = _common_mask(topo, c, [T.cores[d] for d in dests])
+                expect.append(((1, dests.index(rank), x), r, 2 * _count(m)))
+    expect.sort()
+    te.wait_ge(S.q_s, 4)
+    for n, (_, r, cnt) in enumerate(expect):
+        last = n == len(expect) - 1
+        te.wait_ge(S["arr%d" % r], cnt)
+        for i in range(4):
+            mm = te.matmul_mx(T.acc[:, 512 * i:512 * i + W], T.qs[:, W * i:W * i + W], T.ss[:, W * i:W * i + W],
+                              T.land_q[:, W * r:W * r + W], T.land_s[:, W * r:W * r + W], False, last)
+            if last:
+                mm.then_inc(S["fin%d" % i], 1)
+
+    for i in range(4):
+        if i % 2 == 0:
+            v.wait_ge(S["fin%d" % i], 1)
+            v.tensor_copy(T.y_sb[:, i:512:4], T.acc[:, 512 * i:512 * i + W]).then_inc(S.yc, 1)
+        else:
+            sc.wait_ge(S["fin%d" % i], 1)
+            sc.activation(T.y_sb[:, i:512:4], T.acc[:, 512 * i:512 * i + W],
+                          ActivationFunctionType.Copy).then_inc(S.yc, 1)
+    sy.wait_ge(S.yc, 4)
+    sy.dma_start(T.y[:], T.y_sb[:]).then_inc(S.stored, 16)
+    sy.wait_ge(S.stored, 16)
+    g.wait_ge(S.sent, 2 * (_count(lo) + _count(hi)))

@@ -4,7 +4,8 @@ from concourse.mybir import dt, AluOpType, ActivationFunctionType
 N = 12
 SIM_CORES = 256
 W = 128
-NRELAY = 2
+NDIRECT = 4
+OWN0 = 336
 
 SCRATCH = {
     "a_sb": ("sbuf", [128, 2048], "bfloat16"),
@@ -13,10 +14,10 @@ SCRATCH = {
     "sa": ("sbuf", [128, 512], "uint8"),
     "qb": ("sbuf", [128, 128], "float8_e4m3fn_x4"),
     "sb": ("sbuf", [128, 128], "uint8"),
-    "ones": ("sbuf", [128, 516], "bfloat16"),
-    "z": ("sbuf", [128, 516], "bfloat16"),
-    "qs": ("sbuf", [128, 512], "float8_e4m3fn_x4"),
-    "ss": ("sbuf", [128, 512], "uint8"),
+    "ones": ("sbuf", [128, 1024], "bfloat16"),
+    "zt": ("sbuf", [128, 1024], "bfloat16"),
+    "qz": ("sbuf", [128, 512], "float8_e4m3fn_x4"),
+    "sz": ("sbuf", [128, 512], "uint8"),
     "t_sb": ("sbuf", [128, 512], "bfloat16"),
     "qt": ("sbuf", [128, 128], "float8_e4m3fn_x4"),
     "st": ("sbuf", [128, 128], "uint8"),
@@ -26,32 +27,16 @@ SCRATCH = {
     "land_s": ("sbuf", [128, N * 128], "uint8"),
     "y_sb": ("sbuf", [128, 512], "float32"),
     "pp": ("psum", [128, 2048], "float32"),
-    "acc": ("psum", [128, 2048], "float32"),
+    "acc": ("psum", [128, 1024], "float32"),
 }
-SEMAPHORES = (["ld_b", "q_b", "ones_ok", "z_ok", "cp", "q_t", "q_s", "rel_s", "rel_q", "sent", "yc", "stored"]
-              + ["ld_a%d" % i for i in range(4)] + ["q_a%d" % i for i in range(4)]
-              + ["pm%d" % i for i in range(4)] + ["fin%d" % i for i in range(4)]
+SEMAPHORES = (["ld_b", "ld_a0", "ld_a1", "q_b", "q_a0", "q_a1", "ones_ok", "z_ok", "q_z", "sel", "cp", "q_t",
+               "rel_s", "rel_q", "sent", "fin0", "fin1", "yc", "stored"]
+              + ["pm%d" % i for i in range(4)]
               + ["arr%d" % r for r in range(N)])
 
 
 def _count(mask):
     return bin(mask).count("1")
-
-
-def _plan(T, topo, r):
-    me = T.cores[r]
-    near = [d for d in range(N) if d == r or topo.may_write(me, T.cores[d])]
-    far = [d for d in range(N) if d not in near]
-    k = near.index(r)
-    direct = [near[(k + j) % len(near)] for j in range(1, len(near))]
-    far = [far[(k + j) % len(far)] for j in range(len(far))]
-    chip = [c for c in range(SIM_CORES)
-            if c != me and topo.host(c) == topo.host(me) and topo.chip(c) == topo.chip(me)]
-    able = [c for c in chip if all(topo.may_write(c, T.cores[d]) for d in far)]
-    able.sort(key=lambda c: (topo.die(c) == topo.die(me), c))
-    relays = able[:NRELAY] if far else []
-    share = (len(far) + len(relays) - 1) // len(relays) if relays else 0
-    return direct, [(c, far[share * x:share * x + share]) for x, c in enumerate(relays)]
 
 
 def _common_mask(topo, src, dsts):
@@ -69,21 +54,69 @@ def _ids(topo, src, dsts):
     return out
 
 
-def _relay_program(g, core, T, topo, r, dests, n_in):
+def _plan(T, topo, r):
+    me = T.cores[r]
+    near = [d for d in range(N) if d == r or topo.may_write(me, T.cores[d])]
+    far = [d for d in range(N) if d not in near]
+    k = near.index(r)
+    near = [near[(k + j) % len(near)] for j in range(1, len(near))]
+    far = [far[(k + j) % len(far)] for j in range(len(far))]
+    direct, rest = near[:NDIRECT], near[NDIRECT:]
+    chip = [c for c in range(SIM_CORES)
+            if c != me and topo.host(c) == topo.host(me) and topo.chip(c) == topo.chip(me)]
+    able = [c for c in chip if all(topo.may_write(c, T.cores[d]) for d in range(N) if d != r)]
+    other = [c for c in able if topo.die(c) != topo.die(me)]
+    own = [c for c in able if topo.die(c) == topo.die(me)]
+    half = (len(far) + 1) // 2
+    codes = [(other[0], far[:half] + rest), (other[1], far[half:])]
+    order = []
+    for j in range(max(len(codes[0][1]), len(codes[1][1]))):
+        for _, ds in codes:
+            if j < len(ds):
+                order.append(ds[j])
+    return {"direct": direct, "codes": codes, "plane": (own[0], order)}
+
+
+def _make_piece(g, T, c0, c1):
+    wn = c1 - c0
+    g.vector.memset(T.ones[:, 0:4 * wn], 1.0).then_inc(T.sem.ones_ok, 1)
+    g.wait_ge(T.sem.ones_ok, 1)
+    g.affine_select(T.zt[:, 0:4 * wn], T.ones[:, 0:4 * wn], [[1, wn], [-1, 4]], AluOpType.is_equal, 0.0, c0, -4
+                    ).then_inc(T.sem.z_ok, 1)
+
+
+def _relay_program(g, core, T, topo, r, dests, is_plane, n_in, piece):
+    v = g.vector
+    S = T.sem
+    home = T.cores[r]
     cores = [T.cores[d] for d in dests]
     m = _common_mask(topo, core, cores)
+    mh = m & topo.mask(core, home)
+    c0, c1, c2 = piece
+    _make_piece(g, T, c0, c1)
+    v.wait_ge(S.z_ok, 1)
+    v.quantize_mx(T.qz[:, c0:c1], T.sz[:, c0:c1], T.zt[:, 0:4 * (c1 - c0)]).then_inc(S.q_z, 1)
+    g.wait_ge(S.q_z, 1)
+    hid = _ids(topo, core, [home])
+    g.remote_dma_fused([RemoteDMATransfer(dst_ids=hid, dma_engine_mask=mh, remote_sem=S.sel,
+                                          srcs=[T.sz[:, c0:c2]], dsts=[T.sz[:, c0:c2]])], local_sem=S.sent)
+    g.remote_dma_fused([RemoteDMATransfer(dst_ids=hid, dma_engine_mask=mh, remote_sem=S.sel,
+                                          srcs=[T.qz[:, c0:c2].bitcast(dt.uint8)],
+                                          dsts=[T.qz[:, c0:c2].bitcast(dt.uint8)])], local_sem=S.sent)
     ids = _ids(topo, core, cores)
     sl = slice(W * r, W * r + W)
-    g.wait_ge(T.sem.rel_s, n_in)
-    g.remote_dma_fused([RemoteDMATransfer(dst_ids=ids, dma_engine_mask=m, remote_sem=T.sem["arr%d" % r],
-                                          srcs=[T.rs[:]], dsts=[T.land_s[:, sl] for _ in dests])],
-                       local_sem=T.sem.sent)
-    g.wait_ge(T.sem.rel_q, n_in)
-    g.remote_dma_fused([RemoteDMATransfer(dst_ids=ids, dma_engine_mask=m, remote_sem=T.sem["arr%d" % r],
-                                          srcs=[T.rq[:].bitcast(dt.uint8)],
-                                          dsts=[T.land_q[:, sl].bitcast(dt.uint8) for _ in dests])],
-                       local_sem=T.sem.sent)
-    g.wait_ge(T.sem.sent, 2 * _count(m))
+    if is_plane:
+        g.wait_ge(S.rel_s, n_in)
+        g.remote_dma_fused([RemoteDMATransfer(dst_ids=ids, dma_engine_mask=m, remote_sem=S["arr%d" % r],
+                                              srcs=[T.rs[:]], dsts=[T.land_s[:, sl] for _ in dests])],
+                           local_sem=S.sent)
+    else:
+        g.wait_ge(S.rel_q, n_in)
+        g.remote_dma_fused([RemoteDMATransfer(dst_ids=ids, dma_engine_mask=m, remote_sem=S["arr%d" % r],
+                                              srcs=[T.rq[:].bitcast(dt.uint8)],
+                                              dsts=[T.land_q[:, sl].bitcast(dt.uint8) for _ in dests])],
+                           local_sem=S.sent)
+    g.wait_ge(S.sent, 2 * _count(mh) + _count(m))
 
 
 def rank_program(g, core, T, topo):
@@ -92,82 +125,75 @@ def rank_program(g, core, T, topo):
 
     def masks(r):
         me = T.cores[r]
-        direct, relays = plans[r]
-        lo = _common_mask(topo, me, [T.cores[d] for d in direct])
-        on = _common_mask(topo, me, [c for c, _ in relays])
+        p = plans[r]
+        lo = _common_mask(topo, me, [T.cores[d] for d in p["direct"]])
+        on = _common_mask(topo, me, [c for c, _ in p["codes"]] + [p["plane"][0]])
         hi = on & ~lo
         return lo, (hi if hi else on)
 
+    def out_mask(c, dests):
+        return _common_mask(topo, c, [T.cores[d] for d in dests])
+
     if rank is None:
         for r in range(N):
-            for c, dests in plans[r][1]:
+            p = plans[r]
+            n_in = _count(masks(r)[1])
+            for x, (c, dests) in enumerate(p["codes"]):
                 if c == core:
-                    _relay_program(g, core, T, topo, r, dests, _count(masks(r)[1]))
+                    _relay_program(g, core, T, topo, r, dests, False, n_in, (W * x, W * x + W, W * x + W))
+            if p["plane"][0] == core:
+                _relay_program(g, core, T, topo, r, p["plane"][1], True, n_in, (2 * W, 3 * W, OWN0))
         return
 
     v, te, sc, sy = g.vector, g.tensor, g.scalar, g.sync
     S = T.sem
+    plan = plans[rank]
 
     sy.dma_start(T.b_sb[:], T.b[:]).then_inc(S.ld_b, 16)
-    for i in range(4):
-        q = sc if i % 2 == 0 else sy
-        q.dma_start(T.a_sb[:, 512 * i:512 * i + 512], T.a[:, 512 * i:512 * i + 512]).then_inc(S["ld_a%d" % i], 16)
+    sc.dma_start(T.a_sb[:, 0:1024], T.a[:, 0:1024]).then_inc(S.ld_a0, 16)
+    sy.dma_start(T.a_sb[:, 1024:2048], T.a[:, 1024:2048]).then_inc(S.ld_a1, 16)
 
-    v.memset(T.ones[:], 1.0).then_inc(S.ones_ok, 1)
-    g.wait_ge(S.ones_ok, 1)
-    g.affine_select(T.z[:], T.ones[:], [[-1, 516]], AluOpType.is_equal, 0.0, 3, 4).then_inc(S.z_ok, 1)
-
-    def quant_a(i):
-        v.wait_ge(S["ld_a%d" % i], 16)
-        v.quantize_mx(T.qa[:, W * i:W * i + W], T.sa[:, W * i:W * i + W],
-                      T.a_sb[:, 512 * i:512 * i + 512]).then_inc(S["q_a%d" % i], 1)
-
-    def copy_p(i):
-        v.wait_ge(S["pm%d" % i], 1)
-        v.tensor_copy(T.t_sb[:, i:512:4], T.pp[:, 512 * i:512 * i + W]).then_inc(S.cp, 1)
+    _make_piece(g, T, OWN0, 4 * W)
 
     v.wait_ge(S.ld_b, 16)
     v.quantize_mx(T.qb[:], T.sb[:], T.b_sb[:]).then_inc(S.q_b, 1)
-    quant_a(0)
-    quant_a(1)
-    copy_p(0)
-    quant_a(2)
-    copy_p(1)
-    quant_a(3)
-    copy_p(2)
-    copy_p(3)
-    v.wait_ge(S.cp, 4)
-    v.quantize_mx(T.qt[:], T.st[:], T.t_sb[:]).then_inc(S.q_t, 1)
-    v.wait_ge(S.z_ok, 1)
-    for i in range(4):
-        v.quantize_mx(T.qs[:, W * i:W * i + W], T.ss[:, W * i:W * i + W], T.z[:, 3 - i:3 - i + 512]).then_inc(S.q_s, 1)
-
-    def product(out, i, stop):
-        return te.matmul_mx(out[:, 512 * i:512 * i + W], T.qa[:, W * i:W * i + W], T.sa[:, W * i:W * i + W],
-                            T.qb[:], T.sb[:], True, stop)
+    for h in range(2):
+        v.wait_ge(S["ld_a%d" % h], 16)
+        v.quantize_mx(T.qa[:, 2 * W * h:2 * W * h + 2 * W], T.sa[:, 2 * W * h:2 * W * h + 2 * W],
+                      T.a_sb[:, 1024 * h:1024 * h + 1024]).then_inc(S["q_a%d" % h], 1)
 
     te.wait_ge(S.q_b, 1)
     for i in range(4):
-        te.wait_ge(S["q_a%d" % i], 1)
-        product(T.pp, i, True).then_inc(S["pm%d" % i], 1)
-    for i in range(4):
-        product(T.acc, i, False)
+        if i % 2 == 0:
+            te.wait_ge(S["q_a%d" % (i // 2)], 1)
+        te.matmul_mx(T.pp[:, 512 * i:512 * i + W], T.qb[:], T.sb[:],
+                     T.qa[:, W * i:W * i + W], T.sa[:, W * i:W * i + W], True, True).then_inc(S["pm%d" % i], 1)
 
-    direct, relays = plans[rank]
+    for i in range(3):
+        sc.wait_ge(S["pm%d" % i], 1)
+        sc.activation(T.t_sb[:, i:512:4], T.pp[:, 512 * i:512 * i + W], ActivationFunctionType.Copy).then_inc(S.cp, 1)
+    v.wait_ge(S.pm3, 1)
+    v.tensor_copy(T.t_sb[:, 3:512:4], T.pp[:, 1536:1536 + W]).then_inc(S.cp, 1)
+    v.wait_ge(S.cp, 4)
+    v.quantize_mx(T.qt[:], T.st[:], T.t_sb[:]).then_inc(S.q_t, 1)
+    v.wait_ge(S.z_ok, 1)
+    v.quantize_mx(T.qz[:, OWN0:4 * W], T.sz[:, OWN0:4 * W], T.zt[:, 0:4 * (4 * W - OWN0)]).then_inc(S.q_z, 1)
+
     lo, hi = masks(rank)
     sl = slice(W * rank, W * rank + W)
-    dcores = [T.cores[d] for d in direct]
-    rcores = [c for c, _ in relays]
+    dcores = [T.cores[d] for d in plan["direct"]]
+    ccores = [c for c, _ in plan["codes"]]
+    pcore = plan["plane"][0]
     g.wait_ge(S.q_t, 1)
     g.remote_dma_fused([
-        RemoteDMATransfer(dst_ids=_ids(topo, core, rcores), dma_engine_mask=hi, remote_sem=S.rel_s,
-                          srcs=[T.st[:]], dsts=[T.rs[:] for _ in rcores]),
+        RemoteDMATransfer(dst_ids=_ids(topo, core, [pcore]), dma_engine_mask=hi, remote_sem=S.rel_s,
+                          srcs=[T.st[:]], dsts=[T.rs[:]]),
         RemoteDMATransfer(dst_ids=_ids(topo, core, dcores), dma_engine_mask=lo, remote_sem=S["arr%d" % rank],
                           srcs=[T.st[:]], dsts=[T.land_s[:, sl] for _ in dcores]),
     ], local_sem=S.sent)
     g.remote_dma_fused([
-        RemoteDMATransfer(dst_ids=_ids(topo, core, rcores), dma_engine_mask=hi, remote_sem=S.rel_q,
-                          srcs=[T.qt[:].bitcast(dt.uint8)], dsts=[T.rq[:].bitcast(dt.uint8) for _ in rcores]),
+        RemoteDMATransfer(dst_ids=_ids(topo, core, ccores), dma_engine_mask=hi, remote_sem=S.rel_q,
+                          srcs=[T.qt[:].bitcast(dt.uint8)], dsts=[T.rq[:].bitcast(dt.uint8) for _ in ccores]),
         RemoteDMATransfer(dst_ids=_ids(topo, core, dcores), dma_engine_mask=lo, remote_sem=S["arr%d" % rank],
                           srcs=[T.qt[:].bitcast(dt.uint8)], dsts=[T.land_q[:, sl].bitcast(dt.uint8) for _ in dcores]),
     ], local_sem=S.sent)
@@ -176,33 +202,39 @@ def rank_program(g, core, T, topo):
     for r in range(N):
         if r == rank:
             continue
-        d_r, rel_r = plans[r]
-        if rank in d_r:
-            expect.append(((0, d_r.index(rank), 0), r, 2 * _count(masks(r)[0])))
-        for x, (c, dests) in enumerate(rel_r):
+        p = plans[r]
+        if rank in p["direct"]:
+            expect.append(((p["direct"].index(rank), 0), r, 2 * _count(masks(r)[0])))
+        for x, (c, dests) in enumerate(p["codes"]):
             if rank in dests:
-                m = _common_mask(topo, c, [T.cores[d] for d in dests])
-                expect.append(((1, dests.index(rank), x), r, 2 * _count(m)))
+                cnt = _count(out_mask(c, dests)) + _count(out_mask(p["plane"][0], p["plane"][1]))
+                expect.append(((dests.index(rank) + x, 1 + x), r, cnt))
     expect.sort()
-    te.wait_ge(S.q_s, 4)
-    for n, (_, r, cnt) in enumerate(expect):
-        last = n == len(expect) - 1
-        te.wait_ge(S["arr%d" % r], cnt)
-        for i in range(4):
-            mm = te.matmul_mx(T.acc[:, 512 * i:512 * i + W], T.qs[:, W * i:W * i + W], T.ss[:, W * i:W * i + W],
-                              T.land_q[:, W * r:W * r + W], T.land_s[:, W * r:W * r + W], False, last)
-            if last:
-                mm.then_inc(S["fin%d" % i], 1)
 
-    for i in range(4):
-        if i % 2 == 0:
-            v.wait_ge(S["fin%d" % i], 1)
-            v.tensor_copy(T.y_sb[:, i:512:4], T.acc[:, 512 * i:512 * i + W]).then_inc(S.yc, 1)
-        else:
-            sc.wait_ge(S["fin%d" % i], 1)
-            sc.activation(T.y_sb[:, i:512:4], T.acc[:, 512 * i:512 * i + W],
-                          ActivationFunctionType.Copy).then_inc(S.yc, 1)
-    sy.wait_ge(S.yc, 4)
+    n_sel = 0
+    for c, dests in plan["codes"] + [plan["plane"]]:
+        n_sel += 2 * _count(out_mask(c, dests) & topo.mask(c, core))
+
+    def read(q, s, start, stop):
+        for h in range(2):
+            mm = te.matmul_mx(T.acc[:, 512 * h:512 * h + 2 * W], q, s,
+                              T.qz[:, 2 * W * h:2 * W * h + 2 * W], T.sz[:, 2 * W * h:2 * W * h + 2 * W], start, stop)
+            if stop:
+                mm.then_inc(S["fin%d" % h], 1)
+
+    te.wait_ge(S.sel, n_sel)
+    te.wait_ge(S.q_t, 1)
+    te.wait_ge(S.q_z, 1)
+    read(T.qt[:], T.st[:], True, False)
+    for n, (_, r, cnt) in enumerate(expect):
+        te.wait_ge(S["arr%d" % r], cnt)
+        read(T.land_q[:, W * r:W * r + W], T.land_s[:, W * r:W * r + W], False, n == len(expect) - 1)
+
+    v.wait_ge(S.fin0, 1)
+    v.tensor_copy(T.y_sb[:, 0:256], T.acc[:, 0:256]).then_inc(S.yc, 1)
+    sc.wait_ge(S.fin1, 1)
+    sc.activation(T.y_sb[:, 256:512], T.acc[:, 512:768], ActivationFunctionType.Copy).then_inc(S.yc, 1)
+    sy.wait_ge(S.yc, 2)
     sy.dma_start(T.y[:], T.y_sb[:]).then_inc(S.stored, 16)
     sy.wait_ge(S.stored, 16)
     g.wait_ge(S.sent, 2 * (_count(lo) + _count(hi)))

from concourse.bass import DstId, RemoteDMATransfer
from concourse.mybir import dt, AluOpType, ActivationFunctionType

N = 12
SIM_CORES = 256
W = 128
NDIRECT = 4
OWN0 = 336

SCRATCH = {
    "a_sb": ("sbuf", [128, 2048], "bfloat16"),
    "b_sb": ("sbuf", [128, 512], "bfloat16"),
    "qa": ("sbuf", [128, 512], "float8_e4m3fn_x4"),
    "sa": ("sbuf", [128, 512], "uint8"),
    "qb": ("sbuf", [128, 128], "float8_e4m3fn_x4"),
    "sb": ("sbuf", [128, 128], "uint8"),
    "ones": ("sbuf", [128, 1024], "bfloat16"),
    "zt": ("sbuf", [128, 1024], "bfloat16"),
    "qz": ("sbuf", [128, 512], "float8_e4m3fn_x4"),
    "sz": ("sbuf", [128, 512], "uint8"),
    "t_sb": ("sbuf", [128, 512], "bfloat16"),
    "qt": ("sbuf", [128, 128], "float8_e4m3fn_x4"),
    "st": ("sbuf", [128, 128], "uint8"),
    "rq": ("sbuf", [128, 128], "float8_e4m3fn_x4"),
    "rs": ("sbuf", [128, 128], "uint8"),
    "land_q": ("sbuf", [128, N * 128], "float8_e4m3fn_x4"),
    "land_s": ("sbuf", [128, N * 128], "uint8"),
    "y_sb": ("sbuf", [128, 512], "float32"),
    "pp": ("psum", [128, 2048], "float32"),
    "acc": ("psum", [128, 1024], "float32"),
}
SEMAPHORES = (["ld_b", "ld_a0", "ld_a1", "q_b", "q_a0", "q_a1", "ones_ok", "z_ok", "q_z", "sel", "cp", "q_t",
               "rel_s", "rel_q", "sent", "fin0", "fin1", "yc", "stored"]
              + ["pm%d" % i for i in range(4)]
              + ["arr%d" % r for r in range(N)])


def _count(mask):
    return bin(mask).count("1")


def _common_mask(topo, src, dsts):
    m = topo.mask(src, dsts[0])
    for d in dsts[1:]:
        m &= topo.mask(src, d)
    return m


def _ids(topo, src, dsts):
    out = []
    for d in dsts:
        rid, pid = topo.addr(d, src)
        out.append(DstId(rid=rid, pnc=pid))
    return out


def _plan(T, topo, r):
    me = T.cores[r]
    near = [d for d in range(N) if d == r or topo.may_write(me, T.cores[d])]
    far = [d for d in range(N) if d not in near]
    k = near.index(r)
    near = [near[(k + j) % len(near)] for j in range(1, len(near))]
    far = [far[(k + j) % len(far)] for j in range(len(far))]
    direct, rest = near[:NDIRECT], near[NDIRECT:]
    chip = [c for c in range(SIM_CORES)
            if c != me and topo.host(c) == topo.host(me) and topo.chip(c) == topo.chip(me)]
    able = [c for c in chip if all(topo.may_write(c, T.cores[d]) for d in range(N) if d != r)]
    other = [c for c in able if topo.die(c) != topo.die(me)]
    own = [c for c in able if topo.die(c) == topo.die(me)]
    half = (len(far) + 1) // 2
    codes = [(other[0], far[:half] + rest), (other[1], far[half:])]
    order = []
    for j in range(max(len(codes[0][1]), len(codes[1][1]))):
        for _, ds in codes:
            if j < len(ds):
                order.append(ds[j])
    return {"direct": direct, "codes": codes, "plane": (own[0], order)}


def _make_piece(g, T, c0, c1):
    wn = c1 - c0
    g.vector.memset(T.ones[:, 0:4 * wn], 1.0).then_inc(T.sem.ones_ok, 1)
    g.wait_ge(T.sem.ones_ok, 1)
    g.affine_select(T.zt[:, 0:4 * wn], T.ones[:, 0:4 * wn], [[1, wn], [-1, 4]], AluOpType.is_equal, 0.0, c0, -4
                    ).then_inc(T.sem.z_ok, 1)


def _relay_program(g, core, T, topo, r, dests, is_plane, n_in, piece):
    v = g.vector
    S = T.sem
    home = T.cores[r]
    cores = [T.cores[d] for d in dests]
    m = _common_mask(topo, core, cores)
    mh = m & topo.mask(core, home)
    c0, c1, c2 = piece
    _make_piece(g, T, c0, c1)
    v.wait_ge(S.z_ok, 1)
    v.quantize_mx(T.qz[:, c0:c1], T.sz[:, c0:c1], T.zt[:, 0:4 * (c1 - c0)]).then_inc(S.q_z, 1)
    g.wait_ge(S.q_z, 1)
    hid = _ids(topo, core, [home])
    g.remote_dma_fused([RemoteDMATransfer(dst_ids=hid, dma_engine_mask=mh, remote_sem=S.sel,
                                          srcs=[T.sz[:, c0:c2]], dsts=[T.sz[:, c0:c2]])], local_sem=S.sent)
    g.remote_dma_fused([RemoteDMATransfer(dst_ids=hid, dma_engine_mask=mh, remote_sem=S.sel,
                                          srcs=[T.qz[:, c0:c2].bitcast(dt.uint8)],
                                          dsts=[T.qz[:, c0:c2].bitcast(dt.uint8)])], local_sem=S.sent)
    ids = _ids(topo, core, cores)
    sl = slice(W * r, W * r + W)
    if is_plane:
        g.wait_ge(S.rel_s, n_in)
        g.remote_dma_fused([RemoteDMATransfer(dst_ids=ids, dma_engine_mask=m, remote_sem=S["arr%d" % r],
                                              srcs=[T.rs[:]], dsts=[T.land_s[:, sl] for _ in dests])],
                           local_sem=S.sent)
    else:
        g.wait_ge(S.rel_q, n_in)
        g.remote_dma_fused([RemoteDMATransfer(dst_ids=ids, dma_engine_mask=m, remote_sem=S["arr%d" % r],
                                              srcs=[T.rq[:].bitcast(dt.uint8)],
                                              dsts=[T.land_q[:, sl].bitcast(dt.uint8) for _ in dests])],
                           local_sem=S.sent)
    g.wait_ge(S.sent, 2 * _count(mh) + _count(m))


def rank_program(g, core, T, topo):
    rank = T.rank_of(core)
    plans = [_plan(T, topo, r) for r in range(N)]

    def masks(r):
        me = T.cores[r]
        p = plans[r]
        lo = _common_mask(topo, me, [T.cores[d] for d in p["direct"]])
        on = _common_mask(topo, me, [c for c, _ in p["codes"]] + [p["plane"][0]])
        hi = on & ~lo
        return lo, (hi if hi else on)

    def out_mask(c, dests):
        return _common_mask(topo, c, [T.cores[d] for d in dests])

    if rank is None:
        for r in range(N):
            p = plans[r]
            n_in = _count(masks(r)[1])
            for x, (c, dests) in enumerate(p["codes"]):
                if c == core:
                    _relay_program(g, core, T, topo, r, dests, False, n_in, (W * x, W * x + W, W * x + W))
            if p["plane"][0] == core:
                _relay_program(g, core, T, topo, r, p["plane"][1], True, n_in, (2 * W, 3 * W, OWN0))
        return

    v, te, sc, sy = g.vector, g.tensor, g.scalar, g.sync
    S = T.sem
    plan = plans[rank]

    sy.dma_start(T.b_sb[:], T.b[:]).then_inc(S.ld_b, 16)
    sc.dma_start(T.a_sb[:, 0:1024], T.a[:, 0:1024]).then_inc(S.ld_a0, 16)
    sy.dma_start(T.a_sb[:, 1024:2048], T.a[:, 1024:2048]).then_inc(S.ld_a1, 16)

    _make_piece(g, T, OWN0, 4 * W)

    v.wait_ge(S.ld_b, 16)
    v.quantize_mx(T.qb[:], T.sb[:], T.b_sb[:]).then_inc(S.q_b, 1)
    for h in range(2):
        v.wait_ge(S["ld_a%d" % h], 16)
        v.quantize_mx(T.qa[:, 2 * W * h:2 * W * h + 2 * W], T.sa[:, 2 * W * h:2 * W * h + 2 * W],
                      T.a_sb[:, 1024 * h:1024 * h + 1024]).then_inc(S["q_a%d" % h], 1)

    te.wait_ge(S.q_b, 1)
    for i in range(4):
        if i % 2 == 0:
            te.wait_ge(S["q_a%d" % (i // 2)], 1)
        te.matmul_mx(T.pp[:, 512 * i:512 * i + W], T.qb[:], T.sb[:],
                     T.qa[:, W * i:W * i + W], T.sa[:, W * i:W * i + W], True, True).then_inc(S["pm%d" % i], 1)

    for i in range(3):
        sc.wait_ge(S["pm%d" % i], 1)
        sc.activation(T.t_sb[:, i:512:4], T.pp[:, 512 * i:512 * i + W], ActivationFunctionType.Copy).then_inc(S.cp, 1)
    v.wait_ge(S.pm3, 1)
    v.tensor_copy(T.t_sb[:, 3:512:4], T.pp[:, 1536:1536 + W]).then_inc(S.cp, 1)
    v.wait_ge(S.cp, 4)
    v.quantize_mx(T.qt[:], T.st[:], T.t_sb[:]).then_inc(S.q_t, 1)
    v.wait_ge(S.z_ok, 1)
    v.quantize_mx(T.qz[:, OWN0:4 * W], T.sz[:, OWN0:4 * W], T.zt[:, 0:4 * (4 * W - OWN0)]).then_inc(S.q_z, 1)

    lo, hi = masks(rank)
    sl = slice(W * rank, W * rank + W)
    dcores = [T.cores[d] for d in plan["direct"]]
    ccores = [c for c, _ in plan["codes"]]
    pcore = plan["plane"][0]
    g.wait_ge(S.q_t, 1)
    g.remote_dma_fused([
        RemoteDMATransfer(dst_ids=_ids(topo, core, [pcore]), dma_engine_mask=hi, remote_sem=S.rel_s,
                          srcs=[T.st[:]], dsts=[T.rs[:]]),
        RemoteDMATransfer(dst_ids=_ids(topo, core, dcores), dma_engine_mask=lo, remote_sem=S["arr%d" % rank],
                          srcs=[T.st[:]], dsts=[T.land_s[:, sl] for _ in dcores]),
    ], local_sem=S.sent)
    g.remote_dma_fused([
        RemoteDMATransfer(dst_ids=_ids(topo, core, ccores), dma_engine_mask=hi, remote_sem=S.rel_q,
                          srcs=[T.qt[:].bitcast(dt.uint8)], dsts=[T.rq[:].bitcast(dt.uint8) for _ in ccores]),
        RemoteDMATransfer(dst_ids=_ids(topo, core, dcores), dma_engine_mask=lo, remote_sem=S["arr%d" % rank],
                          srcs=[T.qt[:].bitcast(dt.uint8)], dsts=[T.land_q[:, sl].bitcast(dt.uint8) for _ in dcores]),
    ], local_sem=S.sent)

    expect = []
    for r in range(N):
        if r == rank:
            continue
        p = plans[r]
        if rank in p["direct"]:
            expect.append(((p["direct"].index(rank), 0), r, 2 * _count(masks(r)[0])))
        for x, (c, dests) in enumerate(p["codes"]):
            if rank in dests:
                cnt = _count(out_mask(c, dests)) + _count(out_mask(p["plane"][0], p["plane"][1]))
                expect.append(((dests.index(rank) + x, 1 + x), r, cnt))
    expect.sort()

    n_sel = 0
    for c, dests in plan["codes"] + [plan["plane"]]:
        n_sel += 2 * _count(out_mask(c, dests) & topo.mask(c, core))

    def read(q, s, start, stop):
        for h in range(2):
            mm = te.matmul_mx(T.acc[:, 512 * h:512 * h + 2 * W], q, s,
                              T.qz[:, 2 * W * h:2 * W * h + 2 * W], T.sz[:, 2 * W * h:2 * W * h + 2 * W], start, stop)
            if stop:
                mm.then_inc(S["fin%d" % h], 1)

    te.wait_ge(S.sel, n_sel)
    te.wait_ge(S.q_t, 1)
    te.wait_ge(S.q_z, 1)
    read(T.qt[:], T.st[:], True, False)
    for n, (_, r, cnt) in enumerate(expect):
        te.wait_ge(S["arr%d" % r], cnt)
        read(T.land_q[:, W * r:W * r + W], T.land_s[:, W * r:W * r + W], False, n == len(expect) - 1)

    v.wait_ge(S.fin0, 1)
    v.tensor_copy(T.y_sb[:, 0:256], T.acc[:, 0:256]).then_inc(S.yc, 1)
    sc.wait_ge(S.fin1, 1)
    sc.activation(T.y_sb[:, 256:512], T.acc[:, 512:768], ActivationFunctionType.Copy).then_inc(S.yc, 1)
    sy.wait_ge(S.yc, 2)
    sy.dma_start(T.y[:], T.y_sb[:]).then_inc(S.stored, 16)
    sy.wait_ge(S.stored, 16)
    g.wait_ge(S.sent, 2 * (_count(lo) + _count(hi)))
